import numpy as np
import ml_dtypes


def mxq(x, axis, fmt="e4m3"):
    dtype, down = {"e4m3": (ml_dtypes.float8_e4m3fn, 7), "e5m2": (ml_dtypes.float8_e5m2, 14)}[fmt]
    v = np.moveaxis(np.asarray(x, np.float32).astype(ml_dtypes.bfloat16).astype(np.float64), axis, -1)
    blocks = v.reshape(v.shape[:-1] + (-1, 32))
    amax = np.abs(blocks).max(-1, keepdims=True)
    byte = np.maximum(np.where(amax > 0, np.frexp(amax)[1] - 1 + 127, 0) - down, 1)
    scale = np.exp2(byte - 127.0)
    codes = (blocks / scale).astype(np.float32).astype(dtype).astype(np.float64)
    return np.moveaxis((codes * scale).reshape(v.shape), -1, axis)


WIDE = False


def mx_kscale(k):
    if not WIDE:
        return np.ones(k)
    levels = np.array([10, -10, 5, -5, 0])
    if k % 512:
        return np.exp2(np.random.permutation(np.resize(levels, k // 32))).repeat(32)
    a = np.empty((k // 512, 16))
    for p in range(k // 512):
        a[p, :8] = np.random.permutation(np.resize(levels, 8))
        for g in range(8):
            far = levels[np.abs(levels - a[p, g]) >= 10]
            a[p, g + 8] = far[np.random.randint(len(far))]
    return np.exp2(a.ravel()).repeat(32)


def f64(x):
    return np.asarray(x).astype(np.float64)


def striped(idx):
    return np.tile(idx.reshape(-1, 16).T, (8, 1)).astype(np.uint16)


def unstriped(offs):
    return offs[:16].T.reshape(-1).astype(np.int64)


E2M1 = np.array([0.0, 0.5, 1.0, 1.5, 2.0, 3.0, 4.0, 6.0, -0.0, -0.5, -1.0, -1.5, -2.0, -3.0, -4.0, -6.0])


def pack_weight(w, fmt):
    k, n = w.shape
    w = f64(np.asarray(w, np.float32).astype(ml_dtypes.bfloat16)).reshape(k // 32, 32, n)
    amax = np.abs(w).max(1)
    if fmt == "e4m3":
        byte = np.frexp(amax)[1] - 1 + 127 - 7
    else:
        mant, ex = np.frexp(amax / 6.0)
        byte = np.where(mant > 0.5, ex, ex - 1) + 127
    byte = np.clip(np.where(amax > 0, byte, 1), 1, 254)
    scaled = (w * np.exp2(127.0 - byte)[:, None, :]).reshape(k, n).astype(np.float32)
    by_word = np.ascontiguousarray(scaled.reshape(k // 512, 128, 4, n).transpose(0, 1, 3, 2))
    if fmt == "e4m3":
        words = by_word.astype(ml_dtypes.float8_e4m3fn).view(np.uint8)
    else:
        c = by_word.astype(ml_dtypes.float4_e2m1fn).view(np.uint8) & 0xF
        words = (c[..., 0::2] | (c[..., 1::2] << 4)).reshape(k // 512, 128, 2 * n)
    return np.ascontiguousarray(words), np.ascontiguousarray(byte.astype(np.uint8).reshape(k // 512, 16, n))


def unpack_weight(words, scales, fmt):
    g, _, n = scales.shape
    words = np.ascontiguousarray(words).reshape(g, 128, n, -1)
    if fmt == "e4m3":
        vals = words.view(ml_dtypes.float8_e4m3fn).astype(np.float64)
    else:
        nib = np.empty((g, 128, n, 4), np.uint8)
        nib[..., 0::2] = words & 0xF
        nib[..., 1::2] = words >> 4
        vals = E2M1[nib]
    vals = vals * np.repeat(np.exp2(scales.astype(np.float64) - 127.0), 8, axis=1)[..., None]
    return vals.transpose(0, 1, 3, 2).reshape(g * 512, n)


def gelu(v):
    return 0.5 * v * (1.0 + np.tanh(np.sqrt(2.0 / np.pi) * (v + 0.044715 * v**3)))


T, S, P, K, H, N = 4096, 1024, 512, 1024, 1024, 768


def setup_inputs():
    n = np.random.standard_normal
    s = mx_kscale(K)[:, None]
    u = mx_kscale(H)[:, None]
    d = {}
    d["tab_words"], d["tab_scales"] = pack_weight(n((K, T)) * s, "e2m1")
    d["offs"] = striped(np.random.permutation(T)[:S])
    d["pos1"] = striped(np.random.permutation(S)[:P])
    d["pos2"] = striped(np.random.permutation(S)[:P])
    d["w1"] = (0.34 * n((K, H)) / K ** 0.5 / s).astype(np.float32)
    d["climate"] = np.random.uniform(-1.25, 1.25, (H, S)).astype(np.float32)
    d["gain"] = (np.exp(0.3 * n(H)) * u[:, 0]).astype(np.float32)
    d["w4_words"], d["w4_scales"] = pack_weight(2.0 * n((H, N)) / H ** 0.5 / u, "e2m1")
    return d


def reference(tab_words, tab_scales, offs, pos1, pos2, w1, climate, gain, w4_words, w4_scales):
    v = unpack_weight(tab_words, tab_scales, "e2m1")[:, unstriped(offs)]
    phase = (mxq(f64(w1), 0, "e4m3").T @ v) + f64(climate)
    h = np.cos(phase) * f64(gain)[:, None]
    z = h[:, unstriped(pos1)] - 0.5 * h[:, unstriped(pos2)]
    w4 = unpack_weight(w4_words, w4_scales, "e2m1")
    y = w4.T @ mxq(z, 0, "e4m3")
    return np.abs(y)

@@ -1,0 +1,305 @@
+import math
+from contextlib import ExitStack
+
+import concourse.mybir as mybir
+
+T, S, PAIRS, K, H, N = 4096, 1024, 512, 1024, 1024, 768
+FLOPS = 2 * K * H * S + 2 * H * N * PAIRS
+
+F32 = mybir.dt.float32
+BF16 = mybir.dt.bfloat16
+I32 = mybir.dt.int32
+U32 = mybir.dt.uint32
+U16 = mybir.dt.uint16
+U8 = mybir.dt.uint8
+FP8X4 = mybir.dt.float8_e4m3fn_x4
+FP4X4 = mybir.dt.float4_e2m1fn_x4
+ALU = mybir.AluOpType
+ACT = mybir.ActivationFunctionType
+
+P = 128
+PACK = 4
+K_PASS = P * PACK
+BANK = 512
+HALF = PAIRS // 2
+QUARTER = 128
+TURNS = 1.0 / (2.0 * math.pi)
+
+
+def tile_list_crossdating_match_strength_kernel(
+    tc, tab_words, tab_scales, offs, pos1, pos2, w1, climate, gain, w4_words, w4_scales, out
+):
+    nc = tc.nc
+    with ExitStack() as ctx:
+        keep = ctx.enter_context(tc.tile_pool(name="keep", bufs=1))
+        ring = ctx.enter_context(tc.tile_pool(name="ring", bufs=2))
+        psum = ctx.enter_context(tc.psum_pool(name="psum", bufs=1))
+
+        offs_sb = keep.tile([P, S // 16], U16, name="offs_sb")
+        pos1_sb = keep.tile([P, PAIRS // 16], U16, name="pos1_sb")
+        pos2_sb = keep.tile([P, PAIRS // 16], U16, name="pos2_sb")
+        table = [keep.tile([P, T], U16, name=f"table{a}", align_bytes=64) for a in range(2)]
+        table_sc = keep.tile([P, T], U8, name="table_sc", align_bytes=64)
+        v_codes = [keep.tile([P, S], U16, name=f"v_codes{a}", align_bytes=64) for a in range(2)]
+        v_sc = [keep.tile([P, S], U8, name=f"v_sc{a}", align_bytes=64) for a in range(2)]
+        w_raw = {}
+        w_bf = {}
+        w_codes = {}
+        w_sc = {}
+        for b in range(2):
+            for a in range(2):
+                w_bf[a, b] = keep.tile([P, PACK * K_PASS], BF16, name=f"w_bf{a}{b}", align_bytes=64)
+                w_codes[a, b] = keep.tile([P, K_PASS], U32, name=f"w_codes{a}{b}", align_bytes=64)
+                w_sc[a, b] = keep.tile([P, K_PASS], U8, name=f"w_sc{a}{b}", align_bytes=64)
+                for q in range(2):
+                    w_raw[a, b, q] = keep.tile([P, PACK, K_PASS // 2], F32, name=f"w_raw{a}{b}{q}")
+        clim = [keep.tile([P, S], F32, name=f"clim{i}") for i in range(8)]
+        gain_sb = keep.tile([P, 2, PACK], F32, name="gain_sb")
+        w4_sb = keep.tile([P, 2, 2 * N], U8, name="w4_sb", align_bytes=64)
+        w4_sc = keep.tile([P, 2, N], U8, name="w4_sc", align_bytes=64)
+        minus_half = keep.tile([P, PAIRS], F32, name="minus_half")
+        warm = keep.tile([P, 8], F32, name="warm")
+        warm_out = keep.tile([P, 8], F32, name="warm_out")
+        cosines = [keep.tile([P, S], F32, name=f"cosines{i}") for i in range(8)]
+        turns_hi = [keep.tile([P, BANK], I32, name=f"turns_hi{p}") for p in range(4)]
+        z_f32 = [keep.tile([P, PACK, PAIRS], F32, name=f"z_f32{b}") for b in range(2)]
+        z_codes = {}
+        z_sc = {}
+        for b in range(2):
+            for h in range(2):
+                z_codes[b, h] = keep.tile([P, HALF], U32, name=f"z_codes{b}{h}", align_bytes=64)
+                z_sc[b, h] = keep.tile([P, HALF], U8, name=f"z_sc{b}{h}", align_bytes=64)
+
+        nc.gpsimd.memset(table_sc[:].bitcast(I32), 0)
+        nc.vector.memset(warm[:], 0.0)
+        nc.scalar.activation(warm_out[:], warm[:], ACT.Sin)
+        nc.vector.memset(v_sc[1][:].bitcast(I32), 0)
+        nc.vector.memset(w4_sc[:].rearrange("p a n -> p (a n)").bitcast(I32), 0)
+        nc.vector.memset(minus_half[:], -0.5)
+
+        def load_w1(a, b, q):
+            rows = w1[a * K_PASS : (a + 1) * K_PASS, b * K_PASS + q * 256 : b * K_PASS + (q + 1) * 256]
+            nc.sync.dma_start(out=w_raw[a, b, q][:], in_=rows.rearrange("(p j) c -> p j c", j=PACK))
+
+        def load_clim(i):
+            b, t = divmod(i, PACK)
+            rows = climate[b * K_PASS : (b + 1) * K_PASS, :].rearrange("(p t) j -> p t j", t=PACK)
+            nc.sync.dma_start(out=clim[i][:], in_=rows[:, t, :])
+
+        nc.sync.dma_start(offs_sb[:], offs)
+        nc.sync.dma_start(pos1_sb[:], pos1)
+        nc.sync.dma_start(pos2_sb[:], pos2)
+        nc.sync.dma_start(out=gain_sb[:], in_=gain.rearrange("(b p t) -> p b t", b=2, t=PACK))
+        for q in range(4):
+            words = slice(q * 512, (q + 1) * 512)
+            nc.sync.dma_start(out=table[0][:].bitcast(I32)[:, words], in_=tab_words[0].bitcast(I32)[:, words])
+        for quad in range(4):
+            nc.sync.dma_start(
+                out=table_sc[32 * quad : 32 * quad + 8, :].bitcast(I32),
+                in_=tab_scales[:, 4 * quad : 4 * quad + 4, :].bitcast(I32),
+            )
+        nc.sync.dma_start(out=table[1][:].bitcast(I32), in_=tab_words[1].bitcast(I32))
+        for a in range(2):
+            for q in range(2):
+                load_w1(a, 0, q)
+        load_clim(0)
+        load_clim(1)
+        load_clim(2)
+        load_clim(3)
+        for a in range(2):
+            for q in range(2):
+                load_w1(a, 1, q)
+        for i in range(4, 8):
+            load_clim(i)
+        nc.sync.dma_start(out=w4_sb[:].bitcast(I32), in_=w4_words.rearrange("a p c -> p a c").bitcast(I32))
+        for quad in range(4):
+            nc.sync.dma_start(
+                out=w4_sc[32 * quad : 32 * quad + 4, :, :].bitcast(I32),
+                in_=w4_scales[:, 4 * quad : 4 * quad + 4, :].rearrange("a r n -> r a n").bitcast(I32),
+            )
+
+        def cast_w1(a, b, q, on_vector):
+            dst = w_bf[a, b][:].rearrange("p (t m j) -> p m t j", t=PACK, j=PACK)[:, q * 64 : (q + 1) * 64, :, :]
+            src = w_raw[a, b, q][:].rearrange("p j (m t) -> p m t j", t=PACK)
+            if on_vector:
+                nc.vector.tensor_copy(out=dst, in_=src)
+            else:
+                nc.scalar.copy(out=dst, in_=src)
+
+        def quant_w1(a, b):
+            nc.vector.quantize_mx(out=w_codes[a, b][:].bitcast(FP8X4), scales=w_sc[a, b][:], in_=w_bf[a, b][:])
+
+        phase = {}
+        turns = {}
+
+        def add_climate(i):
+            b, t = divmod(i, PACK)
+            for h in range(2):
+                acc = psum.tile([P, BANK], F32, name="acc", tag=f"bank{(2 * i + h) % 4}")
+                cols = slice(h * BANK, (h + 1) * BANK)
+                for a in range(2):
+                    nc.tensor.matmul_mx(
+                        out=acc[:],
+                        lhsT=w_codes[a, b][:, t * P : (t + 1) * P].bitcast(FP8X4),
+                        lhsT_scale=w_sc[a, b][:, t * P : (t + 1) * P],
+                        rhs=v_codes[a][:, cols].bitcast(FP4X4),
+                        rhs_scale=v_sc[a][:, cols],
+                        start=(a == 0),
+                        stop=(a == 1),
+                    )
+                phase[i, h] = ring.tile([P, BANK], F32, name="phase", tag="phase", bufs=6)
+                nc.vector.scalar_tensor_tensor(
+                    out=phase[i, h][:], in0=acc[:], scalar=math.pi / 2, in1=clim[i][:, cols], op0=ALU.add, op1=ALU.add
+                )
+
+        def count_turns(i, h, engine):
+            if h == 0:
+                turns[i, h] = ring.tile([P, BANK], I32, name="turns_lo", tag="turns_lo", bufs=3)
+            else:
+                turns[i, h] = turns_hi[i // 2]
+            engine.tensor_scalar(
+                out=turns[i, h][:], in0=phase[i, h][:], scalar1=TURNS, scalar2=0.0, op0=ALU.mult, op1=ALU.add
+            )
+
+        def cosine(i):
+            b, t = divmod(i, PACK)
+            frac = ring.tile([P, S], F32, name="frac", tag="frac", bufs=3)
+            for h in range(2):
+                nc.vector.scalar_tensor_tensor(
+                    out=frac[:, h * BANK : (h + 1) * BANK],
+                    in0=phase[i, h][:],
+                    scalar=TURNS,
+                    in1=turns[i, h][:],
+                    op0=ALU.mult,
+                    op1=ALU.subtract,
+                )
+            if i == 7:
+                plain = ring.tile([P, S], F32, name="plain", tag="frac", bufs=3)
+                nc.scalar.activation(plain[:], frac[:], ACT.Sin, scale=2.0 * math.pi)
+                nc.scalar.activation(cosines[i][:], plain[:], ACT.Copy, scale=gain_sb[:, b, t : t + 1])
+            else:
+                nc.scalar.activation(cosines[i][:], frac[:], ACT.Sin, scale=2.0 * math.pi)
+
+        def pick(i, lo, hi):
+            b, t = divmod(i, PACK)
+            master = ring.tile([P, PAIRS], F32, name="master", tag="master", bufs=2)
+            width = hi - lo
+            nc.vector.tensor_tensor(
+                master[:, :width], cosines[i][:].indirect(pos2_sb[:, lo // 16 : hi // 16]), minus_half[:, :width], ALU.mult
+            )
+            return master
+
+        def combine(i, lo, hi, master):
+            b, t = divmod(i, PACK)
+            width = hi - lo
+            dst = z_f32[b][:, t, lo:hi]
+            nc.vector.tensor_tensor(dst, cosines[i][:].indirect(pos1_sb[:, lo // 16 : hi // 16]), master[:, :width], ALU.add)
+            if i != 7:
+                nc.scalar.activation(dst, dst, ACT.Copy, scale=gain_sb[:, b, t : t + 1])
+
+        def gather(i, lo, hi):
+            combine(i, lo, hi, pick(i, lo, hi))
+
+        z_bf = {}
+
+        def weave(b, h, on_vector):
+            z_bf[b, h] = ring.tile([P, HALF, PACK], BF16, name="z_bf", tag="z_bf", bufs=3, align_bytes=64)
+            src = z_f32[b][:, :, h * HALF : (h + 1) * HALF].rearrange("p t m -> p m t")
+            if on_vector:
+                nc.vector.tensor_copy(out=z_bf[b, h][:], in_=src)
+            else:
+                nc.scalar.copy(out=z_bf[b, h][:], in_=src)
+
+        def quant_z(b, h):
+            nc.vector.quantize_mx(
+                out=z_codes[b, h][:].bitcast(FP8X4), scales=z_sc[b, h][:], in_=z_bf[b, h][:].rearrange("p m t -> p (m t)")
+            )
+
+        score = {}
+
+        def score_pass(b, h):
+            for pair in range(3):
+                if b == 0:
+                    score[h, pair] = psum.tile([P, 2, HALF], F32, name="score", tag=f"bank{(4 + 3 * h + pair) % 8}")
+                for e in range(2):
+                    n0 = (2 * pair + e) * P
+                    for q in range(2):
+                        cols = slice(q * QUARTER, (q + 1) * QUARTER)
+                        nc.tensor.matmul_mx(
+                            out=score[h, pair][:, e, cols],
+                            lhsT=w4_sb[:, b, 2 * n0 : 2 * (n0 + P)].bitcast(FP4X4),
+                            lhsT_scale=w4_sc[:, b, n0 : n0 + P],
+                            rhs=z_codes[b, h][:, cols].bitcast(FP8X4),
+                            rhs_scale=z_sc[b, h][:, cols],
+                            start=(b == 0 and e == 0 and q == 0),
+                            stop=(b == 1 and e == 1 and q == 1),
+                        )
+                if b == 1:
+                    strength = ring.tile([P, 2, HALF], F32, name="strength", tag="strength", bufs=3)
+                    nc.scalar.activation(strength[:], score[h, pair][:], ACT.Abs)
+                    rows = out[2 * pair * P : (2 * pair + 2) * P, h * HALF : (h + 1) * HALF]
+                    nc.sync.dma_start(out=rows.rearrange("(e p) m -> p e m", e=2), in_=strength[:])
+
+        nc.vector.tensor_copy(v_codes[0][:], table[0][:].indirect(offs_sb[:]))
+        nc.vector.tensor_copy(v_sc[0][:], table_sc[:].indirect(offs_sb[:]))
+        nc.scalar.dma_start(out=v_sc[1][0:112, :].bitcast(I32), in_=v_sc[0][4:116, :].bitcast(I32))
+        nc.vector.tensor_copy(v_codes[1][:], table[1][:].indirect(offs_sb[:]))
+        cast_w1(0, 0, 0, False)
+        cast_w1(0, 0, 1, False)
+        cast_w1(1, 0, 0, False)
+        quant_w1(0, 0)
+        cast_w1(1, 0, 1, True)
+        quant_w1(1, 0)
+
+        def climate_pair(p):
+            if p > 0:
+                count_turns(2 * p - 1, 1, nc.gpsimd)
+            add_climate(2 * p)
+            add_climate(2 * p + 1)
+            count_turns(2 * p, 0, nc.gpsimd)
+            count_turns(2 * p, 1, nc.gpsimd)
+            count_turns(2 * p + 1, 0, nc.gpsimd)
+
+        climate_pair(0)
+        cosine(0)
+        climate_pair(1)
+        cast_w1(0, 1, 0, False)
+        cast_w1(0, 1, 1, False)
+        cosine(1)
+        cast_w1(1, 1, 0, False)
+        cast_w1(1, 1, 1, False)
+        gather(0, 0, PAIRS)
+        quant_w1(0, 1)
+        gather(1, 0, PAIRS)
+        quant_w1(1, 1)
+        cosine(2)
+        climate_pair(2)
+        cosine(3)
+        gather(2, 0, PAIRS)
+        cosine(4)
+        climate_pair(3)
+        cosine(5)
+        gather(3, 0, PAIRS)
+        cosine(6)
+        count_turns(7, 1, nc.vector)
+        weave(0, 0, False)
+        gather(4, 0, HALF)
+        cosine(7)
+        weave(0, 1, False)
+        gather(5, 0, HALF)
+        quant_z(0, 0)
+        gather(6, 0, HALF)
+        quant_z(0, 1)
+        score_pass(0, 0)
+        score_pass(0, 1)
+        gather(7, 0, HALF)
+        weave(1, 0, False)
+        gather(4, HALF, PAIRS)
+        gather(5, HALF, PAIRS)
+        quant_z(1, 0)
+        score_pass(1, 0)
+        gather(6, HALF, PAIRS)
+        gather(7, HALF, PAIRS)
+        weave(1, 1, True)
+        quant_z(1, 1)
+        score_pass(1, 1)

@@ -23,6 +23,7 @@ K_PASS = P * PACK
 BANK = 512
 HALF = PAIRS // 2
 QUARTER = 128
+PARTS = [(0, 256), (256, 384), (384, 512)]
 TURNS = 1.0 / (2.0 * math.pi)
 
 
@@ -38,8 +39,8 @@ def tile_list_crossdating_match_strength_kernel(
         offs_sb = keep.tile([P, S // 16], U16, name="offs_sb")
         pos1_sb = keep.tile([P, PAIRS // 16], U16, name="pos1_sb")
         pos2_sb = keep.tile([P, PAIRS // 16], U16, name="pos2_sb")
-        table = [keep.tile([P, T], U16, name=f"table{a}", align_bytes=64) for a in range(2)]
-        table_sc = keep.tile([P, T], U8, name="table_sc", align_bytes=64)
+        table = [keep.tile([P, T], U16, name=f"table{a}", tag=f"table{a}", align_bytes=64) for a in range(2)]
+        table_sc = keep.tile([P, T], U8, name="table_sc", tag="table_sc", align_bytes=64)
         v_codes = [keep.tile([P, S], U16, name=f"v_codes{a}", align_bytes=64) for a in range(2)]
         v_sc = [keep.tile([P, S], U8, name=f"v_sc{a}", align_bytes=64) for a in range(2)]
         w_raw = {}
@@ -48,27 +49,23 @@ def tile_list_crossdating_match_strength_kernel(
         w_sc = {}
         for b in range(2):
             for a in range(2):
-                w_bf[a, b] = keep.tile([P, PACK * K_PASS], BF16, name=f"w_bf{a}{b}", align_bytes=64)
+                w_bf[a, b] = keep.tile([P, PACK * K_PASS], BF16, name=f"w_bf{a}{b}", tag=f"w_bf{a}{b}", align_bytes=64)
                 w_codes[a, b] = keep.tile([P, K_PASS], U32, name=f"w_codes{a}{b}", align_bytes=64)
                 w_sc[a, b] = keep.tile([P, K_PASS], U8, name=f"w_sc{a}{b}", align_bytes=64)
-                for q in range(2):
-                    w_raw[a, b, q] = keep.tile([P, PACK, K_PASS // 2], F32, name=f"w_raw{a}{b}{q}")
-        clim = [keep.tile([P, S], F32, name=f"clim{i}") for i in range(8)]
+        clim = {}
         gain_sb = keep.tile([P, 2, PACK], F32, name="gain_sb")
-        w4_sb = keep.tile([P, 2, 2 * N], U8, name="w4_sb", align_bytes=64)
         w4_sc = keep.tile([P, 2, N], U8, name="w4_sc", align_bytes=64)
         minus_half = keep.tile([P, PAIRS], F32, name="minus_half")
         warm = keep.tile([P, 8], F32, name="warm")
         warm_out = keep.tile([P, 8], F32, name="warm_out")
         cosines = [keep.tile([P, S], F32, name=f"cosines{i}") for i in range(8)]
-        turns_hi = [keep.tile([P, BANK], I32, name=f"turns_hi{p}") for p in range(4)]
         z_f32 = [keep.tile([P, PACK, PAIRS], F32, name=f"z_f32{b}") for b in range(2)]
         z_codes = {}
         z_sc = {}
-        for b in range(2):
-            for h in range(2):
-                z_codes[b, h] = keep.tile([P, HALF], U32, name=f"z_codes{b}{h}", align_bytes=64)
-                z_sc[b, h] = keep.tile([P, HALF], U8, name=f"z_sc{b}{h}", align_bytes=64)
+        z_bf = {}
+        for b, lo, hi in [(0, 0, PAIRS)] + [(1, lo, hi) for lo, hi in PARTS]:
+            z_codes[b, lo] = keep.tile([P, hi - lo], U32, name=f"z_codes{b}{lo}", align_bytes=64)
+            z_sc[b, lo] = keep.tile([P, hi - lo], U8, name=f"z_sc{b}{lo}", align_bytes=64)
 
         nc.gpsimd.memset(table_sc[:].bitcast(I32), 0)
         nc.vector.memset(warm[:], 0.0)
@@ -77,14 +74,18 @@ def tile_list_crossdating_match_strength_kernel(
         nc.vector.memset(w4_sc[:].rearrange("p a n -> p (a n)").bitcast(I32), 0)
         nc.vector.memset(minus_half[:], -0.5)
 
-        def load_w1(a, b, q):
+        def load_w1(a, b, q, tag):
+            w_raw[a, b, q] = keep.tile([P, PACK, K_PASS // 2], F32, name="w_raw", tag=tag, align_bytes=64)
             rows = w1[a * K_PASS : (a + 1) * K_PASS, b * K_PASS + q * 256 : b * K_PASS + (q + 1) * 256]
             nc.sync.dma_start(out=w_raw[a, b, q][:], in_=rows.rearrange("(p j) c -> p j c", j=PACK))
 
-        def load_clim(i):
+        def load_clim(i, count, tag):
             b, t = divmod(i, PACK)
             rows = climate[b * K_PASS : (b + 1) * K_PASS, :].rearrange("(p t) j -> p t j", t=PACK)
-            nc.sync.dma_start(out=clim[i][:], in_=rows[:, t, :])
+            staged = keep.tile([P, count, S], F32, name="staged", tag=tag, align_bytes=64)
+            nc.sync.dma_start(out=staged[:], in_=rows[:, t : t + count, :])
+            for e in range(count):
+                clim[i + e] = staged[:, e, :]
 
         nc.sync.dma_start(offs_sb[:], offs)
         nc.sync.dma_start(pos1_sb[:], pos1)
@@ -98,25 +99,11 @@ def tile_list_crossdating_match_strength_kernel(
                 out=table_sc[32 * quad : 32 * quad + 8, :].bitcast(I32),
                 in_=tab_scales[:, 4 * quad : 4 * quad + 4, :].bitcast(I32),
             )
+        load_w1(0, 0, 0, "w_raw00")
+        load_w1(0, 0, 1, "w_raw01")
         nc.sync.dma_start(out=table[1][:].bitcast(I32), in_=tab_words[1].bitcast(I32))
-        for a in range(2):
-            for q in range(2):
-                load_w1(a, 0, q)
-        load_clim(0)
-        load_clim(1)
-        load_clim(2)
-        load_clim(3)
-        for a in range(2):
-            for q in range(2):
-                load_w1(a, 1, q)
-        for i in range(4, 8):
-            load_clim(i)
-        nc.sync.dma_start(out=w4_sb[:].bitcast(I32), in_=w4_words.rearrange("a p c -> p a c").bitcast(I32))
-        for quad in range(4):
-            nc.sync.dma_start(
-                out=w4_sc[32 * quad : 32 * quad + 4, :, :].bitcast(I32),
-                in_=w4_scales[:, 4 * quad : 4 * quad + 4, :].rearrange("a r n -> r a n").bitcast(I32),
-            )
+        load_w1(1, 0, 0, "w_raw10")
+        load_w1(1, 0, 1, "w_raw11")
 
         def cast_w1(a, b, q, on_vector):
             dst = w_bf[a, b][:].rearrange("p (t m j) -> p m t j", t=PACK, j=PACK)[:, q * 64 : (q + 1) * 64, :, :]
@@ -126,14 +113,21 @@ def tile_list_crossdating_match_strength_kernel(
             else:
                 nc.scalar.copy(out=dst, in_=src)
 
-        def quant_w1(a, b):
-            nc.vector.quantize_mx(out=w_codes[a, b][:].bitcast(FP8X4), scales=w_sc[a, b][:], in_=w_bf[a, b][:])
+        def quant_w1(a, b, pieces=1):
+            width = K_PASS // pieces
+            for lo in range(0, K_PASS, width):
+                nc.vector.quantize_mx(
+                    out=w_codes[a, b][:, lo : lo + width].bitcast(FP8X4),
+                    scales=w_sc[a, b][:, lo : lo + width],
+                    in_=w_bf[a, b][:, PACK * lo : PACK * (lo + width)],
+                )
 
         phase = {}
         turns = {}
 
         def add_climate(i):
             b, t = divmod(i, PACK)
+            phase[i] = ring.tile([P, S], F32, name="phase", tag="phase", bufs=3)
             for h in range(2):
                 acc = psum.tile([P, BANK], F32, name="acc", tag=f"bank{(2 * i + h) % 4}")
                 cols = slice(h * BANK, (h + 1) * BANK)
@@ -147,32 +141,22 @@ def tile_list_crossdating_match_strength_kernel(
                         start=(a == 0),
                         stop=(a == 1),
                     )
-                phase[i, h] = ring.tile([P, BANK], F32, name="phase", tag="phase", bufs=6)
                 nc.vector.scalar_tensor_tensor(
-                    out=phase[i, h][:], in0=acc[:], scalar=math.pi / 2, in1=clim[i][:, cols], op0=ALU.add, op1=ALU.add
+                    out=phase[i][:, cols], in0=acc[:], scalar=math.pi / 2, in1=clim[i][:, cols], op0=ALU.add, op1=ALU.add
                 )
 
-        def count_turns(i, h, engine):
-            if h == 0:
-                turns[i, h] = ring.tile([P, BANK], I32, name="turns_lo", tag="turns_lo", bufs=3)
-            else:
-                turns[i, h] = turns_hi[i // 2]
-            engine.tensor_scalar(
-                out=turns[i, h][:], in0=phase[i, h][:], scalar1=TURNS, scalar2=0.0, op0=ALU.mult, op1=ALU.add
+        def count_turns(i):
+            turns[i] = ring.tile([P, S], I32, name="turns", tag="turns", bufs=2)
+            nc.vector.tensor_scalar(
+                out=turns[i][:], in0=phase[i][:], scalar1=TURNS, scalar2=0.0, op0=ALU.mult, op1=ALU.add
             )
 
         def cosine(i):
             b, t = divmod(i, PACK)
             frac = ring.tile([P, S], F32, name="frac", tag="frac", bufs=3)
-            for h in range(2):
-                nc.vector.scalar_tensor_tensor(
-                    out=frac[:, h * BANK : (h + 1) * BANK],
-                    in0=phase[i, h][:],
-                    scalar=TURNS,
-                    in1=turns[i, h][:],
-                    op0=ALU.mult,
-                    op1=ALU.subtract,
-                )
+            nc.vector.scalar_tensor_tensor(
+                out=frac[:], in0=phase[i][:], scalar=TURNS, in1=turns[i][:], op0=ALU.mult, op1=ALU.subtract
+            )
             if i == 7:
                 plain = ring.tile([P, S], F32, name="plain", tag="frac", bufs=3)
                 nc.scalar.activation(plain[:], frac[:], ACT.Sin, scale=2.0 * math.pi)
@@ -180,126 +164,154 @@ def tile_list_crossdating_match_strength_kernel(
             else:
                 nc.scalar.activation(cosines[i][:], frac[:], ACT.Sin, scale=2.0 * math.pi)
 
-        def pick(i, lo, hi):
-            b, t = divmod(i, PACK)
-            master = ring.tile([P, PAIRS], F32, name="master", tag="master", bufs=2)
-            width = hi - lo
-            nc.vector.tensor_tensor(
-                master[:, :width], cosines[i][:].indirect(pos2_sb[:, lo // 16 : hi // 16]), minus_half[:, :width], ALU.mult
-            )
-            return master
+        master = {}
 
-        def combine(i, lo, hi, master):
+        def pick(i, lo, hi, after=None):
+            if after is None:
+                master[i, lo] = ring.tile([P, PAIRS], F32, name="master", tag="master", bufs=3)
+            else:
+                master[i, lo] = keep.tile([P, hi - lo], F32, name="master_late", tag=after, align_bytes=64)
+            nc.vector.tensor_tensor(
+                master[i, lo][:, : hi - lo],
+                cosines[i][:].indirect(pos2_sb[:, lo // 16 : hi // 16]),
+                minus_half[:, : hi - lo],
+                ALU.mult,
+            )
+
+        def combine(i, lo, hi):
             b, t = divmod(i, PACK)
-            width = hi - lo
             dst = z_f32[b][:, t, lo:hi]
-            nc.vector.tensor_tensor(dst, cosines[i][:].indirect(pos1_sb[:, lo // 16 : hi // 16]), master[:, :width], ALU.add)
+            nc.vector.tensor_tensor(
+                dst, cosines[i][:].indirect(pos1_sb[:, lo // 16 : hi // 16]), master[i, lo][:, : hi - lo], ALU.add
+            )
             if i != 7:
                 nc.scalar.activation(dst, dst, ACT.Copy, scale=gain_sb[:, b, t : t + 1])
 
-        def gather(i, lo, hi):
-            combine(i, lo, hi, pick(i, lo, hi))
+        def weave(b, lo, hi, on_vector):
+            z_bf[b, lo] = keep.tile([P, hi - lo, PACK], BF16, name="z_bf", tag=f"z_bf{b}{lo}", align_bytes=64)
+            for m0 in range(lo, hi, HALF):
+                m1 = min(hi, m0 + HALF)
+                src = z_f32[b][:, :, m0:m1].rearrange("p t m -> p m t")
+                if on_vector:
+                    nc.vector.tensor_copy(out=z_bf[b, lo][:, m0 - lo : m1 - lo, :], in_=src)
+                else:
+                    nc.scalar.copy(out=z_bf[b, lo][:, m0 - lo : m1 - lo, :], in_=src)
 
-        z_bf = {}
-
-        def weave(b, h, on_vector):
-            z_bf[b, h] = ring.tile([P, HALF, PACK], BF16, name="z_bf", tag="z_bf", bufs=3, align_bytes=64)
-            src = z_f32[b][:, :, h * HALF : (h + 1) * HALF].rearrange("p t m -> p m t")
-            if on_vector:
-                nc.vector.tensor_copy(out=z_bf[b, h][:], in_=src)
-            else:
-                nc.scalar.copy(out=z_bf[b, h][:], in_=src)
-
-        def quant_z(b, h):
+        def quant_z(b, lo):
             nc.vector.quantize_mx(
-                out=z_codes[b, h][:].bitcast(FP8X4), scales=z_sc[b, h][:], in_=z_bf[b, h][:].rearrange("p m t -> p (m t)")
+                out=z_codes[b, lo][:].bitcast(FP8X4),
+                scales=z_sc[b, lo][:],
+                in_=z_bf[b, lo][:].rearrange("p m t -> p (m t)"),
             )
 
         score = {}
+        first_bank = {0: 4, 256: 7, 384: 1}
 
-        def score_pass(b, h):
-            for pair in range(3):
+        def score_pass(b, lo, hi):
+            per_bank = 2 if hi - lo == 256 else 3
+            base = 0 if b == 0 else lo
+            for g in range(N // P // per_bank):
                 if b == 0:
-                    score[h, pair] = psum.tile([P, 2, HALF], F32, name="score", tag=f"bank{(4 + 3 * h + pair) % 8}")
-                for e in range(2):
-                    n0 = (2 * pair + e) * P
-                    for q in range(2):
-                        cols = slice(q * QUARTER, (q + 1) * QUARTER)
+                    score[lo, g] = psum.tile(
+                        [P, per_bank, hi - lo], F32, name="score", tag=f"bank{(first_bank[lo] + g) % 8}"
+                    )
+                for e in range(per_bank):
+                    n0 = (per_bank * g + e) * P
+                    for m0 in range(lo, hi, QUARTER):
+                        cols = slice(m0 - base, m0 - base + QUARTER)
                         nc.tensor.matmul_mx(
-                            out=score[h, pair][:, e, cols],
+                            out=score[lo, g][:, e, m0 - lo : m0 - lo + QUARTER],
                             lhsT=w4_sb[:, b, 2 * n0 : 2 * (n0 + P)].bitcast(FP4X4),
                             lhsT_scale=w4_sc[:, b, n0 : n0 + P],
-                            rhs=z_codes[b, h][:, cols].bitcast(FP8X4),
-                            rhs_scale=z_sc[b, h][:, cols],
-                            start=(b == 0 and e == 0 and q == 0),
-                            stop=(b == 1 and e == 1 and q == 1),
+                            rhs=z_codes[b, base][:, cols].bitcast(FP8X4),
+                            rhs_scale=z_sc[b, base][:, cols],
+                            start=(b == 0 and e == 0 and m0 == lo),
+                            stop=(b == 1 and e == per_bank - 1 and m0 + QUARTER == hi),
                         )
                 if b == 1:
-                    strength = ring.tile([P, 2, HALF], F32, name="strength", tag="strength", bufs=3)
-                    nc.scalar.activation(strength[:], score[h, pair][:], ACT.Abs)
-                    rows = out[2 * pair * P : (2 * pair + 2) * P, h * HALF : (h + 1) * HALF]
-                    nc.sync.dma_start(out=rows.rearrange("(e p) m -> p e m", e=2), in_=strength[:])
+                    strength = ring.tile([P, per_bank, hi - lo], F32, name="strength", tag="strength", bufs=4)
+                    nc.scalar.activation(strength[:], score[lo, g][:], ACT.Abs)
+                    rows = out[per_bank * g * P : per_bank * (g + 1) * P, lo:hi]
+                    nc.sync.dma_start(out=rows.rearrange("(e p) m -> p e m", e=per_bank), in_=strength[:])
 
         nc.vector.tensor_copy(v_codes[0][:], table[0][:].indirect(offs_sb[:]))
         nc.vector.tensor_copy(v_sc[0][:], table_sc[:].indirect(offs_sb[:]))
-        nc.scalar.dma_start(out=v_sc[1][0:112, :].bitcast(I32), in_=v_sc[0][4:116, :].bitcast(I32))
-        nc.vector.tensor_copy(v_codes[1][:], table[1][:].indirect(offs_sb[:]))
+        nc.sync.dma_start(out=v_sc[1][0:112, :].bitcast(I32), in_=v_sc[0][4:116, :].bitcast(I32))
+        load_clim(0, 1, "table_sc")
         cast_w1(0, 0, 0, False)
+        load_clim(1, 1, "w_raw00")
         cast_w1(0, 0, 1, False)
-        cast_w1(1, 0, 0, False)
         quant_w1(0, 0)
+        nc.vector.tensor_copy(v_codes[1][:], table[1][:].indirect(offs_sb[:]))
+        load_clim(2, 2, "table1")
+        cast_w1(1, 0, 0, False)
         cast_w1(1, 0, 1, True)
-        quant_w1(1, 0)
+        quant_w1(1, 0, 2)
+        load_w1(0, 1, 0, "w_bf00")
+        load_w1(0, 1, 1, "w_raw01")
+        load_w1(1, 1, 0, "w_raw10")
+        load_w1(1, 1, 1, "w_raw11")
+        w4_sb = keep.tile([P, 2, 2 * N], U8, name="w4_sb", tag="w_bf10", align_bytes=64)
 
-        def climate_pair(p):
-            if p > 0:
-                count_turns(2 * p - 1, 1, nc.gpsimd)
-            add_climate(2 * p)
-            add_climate(2 * p + 1)
-            count_turns(2 * p, 0, nc.gpsimd)
-            count_turns(2 * p, 1, nc.gpsimd)
-            count_turns(2 * p + 1, 0, nc.gpsimd)
+        def step(i):
+            add_climate(i)
+            if i > 0:
+                cosine(i - 1)
+            count_turns(i)
 
-        climate_pair(0)
-        cosine(0)
-        climate_pair(1)
+        step(0)
+        load_clim(4, 2, "table_sc")
+        step(1)
         cast_w1(0, 1, 0, False)
         cast_w1(0, 1, 1, False)
-        cosine(1)
+        step(2)
         cast_w1(1, 1, 0, False)
         cast_w1(1, 1, 1, False)
-        gather(0, 0, PAIRS)
+        step(3)
+        load_clim(6, 2, "table1")
+        nc.sync.dma_start(out=w4_sb[:].bitcast(I32), in_=w4_words.rearrange("a p c -> p a c").bitcast(I32))
+        for quad in range(4):
+            nc.sync.dma_start(
+                out=w4_sc[32 * quad : 32 * quad + 4, :, :].bitcast(I32),
+                in_=w4_scales[:, 4 * quad : 4 * quad + 4, :].rearrange("a r n -> r a n").bitcast(I32),
+            )
+        pick(0, 0, PAIRS)
         quant_w1(0, 1)
-        gather(1, 0, PAIRS)
+        combine(0, 0, PAIRS)
         quant_w1(1, 1)
-        cosine(2)
-        climate_pair(2)
-        cosine(3)
-        gather(2, 0, PAIRS)
-        cosine(4)
-        climate_pair(3)
-        cosine(5)
-        gather(3, 0, PAIRS)
-        cosine(6)
-        count_turns(7, 1, nc.vector)
-        weave(0, 0, False)
-        gather(4, 0, HALF)
-        cosine(7)
-        weave(0, 1, False)
-        gather(5, 0, HALF)
-        quant_z(0, 0)
-        gather(6, 0, HALF)
-        quant_z(0, 1)
-        score_pass(0, 0)
-        score_pass(0, 1)
-        gather(7, 0, HALF)
-        weave(1, 0, False)
-        gather(4, HALF, PAIRS)
-        gather(5, HALF, PAIRS)
-        quant_z(1, 0)
-        score_pass(1, 0)
-        gather(6, HALF, PAIRS)
-        gather(7, HALF, PAIRS)
-        weave(1, 1, True)
-        quant_z(1, 1)
-        score_pass(1, 1)
+        for i in range(4, 7):
+            pick(i - 3, 0, PAIRS)
+            add_climate(i)
+            combine(i - 3, 0, PAIRS)
+            cosine(i - 1)
+            count_turns(i)
+        weave(0, 0, PAIRS, False)
+        step(7)
+        work = [(i, lo, hi) for lo, hi in PARTS for i in range(4, 8)]
+        waits = {3: "z_bf00", 8: "z_bf10", 11: "z_bf1256"}
+        last = None
+        for n, item in enumerate(work):
+            if n == 3:
+                quant_z(0, 0)
+                for lo, hi in PARTS:
+                    score_pass(0, lo, hi)
+            if n == 8:
+                quant_z(1, 0)
+                score_pass(1, *PARTS[0])
+            if n == 11:
+                quant_z(1, 256)
+                score_pass(1, *PARTS[1])
+            pick(*item, after=waits.get(n))
+            if n == 0:
+                cosine(7)
+            else:
+                combine(*last)
+            last = item
+            if n == 4:
+                weave(1, *PARTS[0], False)
+            if n == 8:
+                weave(1, *PARTS[1], False)
+        combine(*last)
+        weave(1, *PARTS[2], True)
+        quant_z(1, 384)
+        score_pass(1, *PARTS[2])

@@ -67,24 +67,28 @@ def tile_list_crossdating_match_strength_kernel(
             z_codes[b, lo] = keep.tile([P, hi - lo], U32, name=f"z_codes{b}{lo}", align_bytes=64)
             z_sc[b, lo] = keep.tile([P, hi - lo], U8, name=f"z_sc{b}{lo}", align_bytes=64)
 
-        nc.gpsimd.memset(table_sc[:].bitcast(I32), 0)
+        nc.vector.memset(table_sc[:].bitcast(I32), 0)
         nc.vector.memset(warm[:], 0.0)
         nc.scalar.activation(warm_out[:], warm[:], ACT.Sin)
         nc.vector.memset(v_sc[1][:].bitcast(I32), 0)
         nc.vector.memset(w4_sc[:].rearrange("p a n -> p (a n)").bitcast(I32), 0)
         nc.vector.memset(minus_half[:], -0.5)
 
-        def load_w1(a, b, q, tag):
-            w_raw[a, b, q] = keep.tile([P, PACK, K_PASS // 2], F32, name="w_raw", tag=tag, align_bytes=64)
-            rows = w1[a * K_PASS : (a + 1) * K_PASS, b * K_PASS + q * 256 : b * K_PASS + (q + 1) * 256]
-            nc.sync.dma_start(out=w_raw[a, b, q][:], in_=rows.rearrange("(p j) c -> p j c", j=PACK))
+        def load_w1(a, b, lo, hi, tag):
+            w_raw[a, b, lo] = keep.tile([P, PACK, hi - lo], F32, name="w_raw", tag=tag, align_bytes=64)
+            rows = w1[a * K_PASS : (a + 1) * K_PASS, b * K_PASS + lo : b * K_PASS + hi]
+            nc.sync.dma_start(out=w_raw[a, b, lo][:], in_=rows.rearrange("(p j) c -> p j c", j=PACK))
 
-        def load_clim(i, count, tag):
+        def load_clim(i, tag, split):
             b, t = divmod(i, PACK)
             rows = climate[b * K_PASS : (b + 1) * K_PASS, :].rearrange("(p t) j -> p t j", t=PACK)
-            staged = keep.tile([P, count, S], F32, name="staged", tag=tag, align_bytes=64)
-            nc.sync.dma_start(out=staged[:], in_=rows[:, t : t + count, :])
-            for e in range(count):
+            staged = keep.tile([P, 2, S], F32, name="staged", tag=tag, align_bytes=64)
+            if split:
+                for e in range(2):
+                    nc.sync.dma_start(out=staged[:, e, :], in_=rows[:, t + e, :])
+            else:
+                nc.sync.dma_start(out=staged[:], in_=rows[:, t : t + 2, :])
+            for e in range(2):
                 clim[i + e] = staged[:, e, :]
 
         nc.sync.dma_start(offs_sb[:], offs)
@@ -94,20 +98,19 @@ def tile_list_crossdating_match_strength_kernel(
         for q in range(4):
             words = slice(q * 512, (q + 1) * 512)
             nc.sync.dma_start(out=table[0][:].bitcast(I32)[:, words], in_=tab_words[0].bitcast(I32)[:, words])
-        for quad in range(4):
+        for r in range(4):
             nc.sync.dma_start(
-                out=table_sc[32 * quad : 32 * quad + 8, :].bitcast(I32),
-                in_=tab_scales[:, 4 * quad : 4 * quad + 4, :].bitcast(I32),
+                out=table_sc[r:P:16, :].bitcast(I32),
+                in_=tab_scales.rearrange("a (q r) t -> r q a t", r=4)[r].bitcast(I32),
             )
-        load_w1(0, 0, 0, "w_raw00")
-        load_w1(0, 0, 1, "w_raw01")
+        load_w1(0, 0, 0, K_PASS, "w_raw0")
         nc.sync.dma_start(out=table[1][:].bitcast(I32), in_=tab_words[1].bitcast(I32))
-        load_w1(1, 0, 0, "w_raw10")
-        load_w1(1, 0, 1, "w_raw11")
+        load_w1(1, 0, 0, 256, "w_raw10")
+        load_w1(1, 0, 256, K_PASS, "w_raw11")
 
-        def cast_w1(a, b, q, on_vector):
-            dst = w_bf[a, b][:].rearrange("p (t m j) -> p m t j", t=PACK, j=PACK)[:, q * 64 : (q + 1) * 64, :, :]
-            src = w_raw[a, b, q][:].rearrange("p j (m t) -> p m t j", t=PACK)
+        def cast_w1(a, b, lo, hi, on_vector, base=0):
+            dst = w_bf[a, b][:].rearrange("p (t m j) -> p m t j", t=PACK, j=PACK)[:, lo // PACK : hi // PACK, :, :]
+            src = w_raw[a, b, base][:, :, lo - base : hi - base].rearrange("p j (m t) -> p m t j", t=PACK)
             if on_vector:
                 nc.vector.tensor_copy(out=dst, in_=src)
             else:
@@ -236,22 +239,17 @@ def tile_list_crossdating_match_strength_kernel(
 
         nc.vector.tensor_copy(v_codes[0][:], table[0][:].indirect(offs_sb[:]))
         nc.vector.tensor_copy(v_sc[0][:], table_sc[:].indirect(offs_sb[:]))
-        nc.sync.dma_start(out=v_sc[1][0:112, :].bitcast(I32), in_=v_sc[0][4:116, :].bitcast(I32))
-        load_clim(0, 1, "table_sc")
-        cast_w1(0, 0, 0, False)
-        load_clim(1, 1, "w_raw00")
-        cast_w1(0, 0, 1, False)
+        nc.sync.dma_start(out=v_sc[1][0:112, :].bitcast(I32), in_=v_sc[0][16:128, :].bitcast(I32))
+        load_clim(0, "table_sc", True)
+        cast_w1(0, 0, 0, K_PASS, False)
+        load_clim(2, "w_raw0", True)
         quant_w1(0, 0)
+        load_w1(1, 1, 0, K_PASS, "w_bf00")
         nc.vector.tensor_copy(v_codes[1][:], table[1][:].indirect(offs_sb[:]))
-        load_clim(2, 2, "table1")
-        cast_w1(1, 0, 0, False)
-        cast_w1(1, 0, 1, True)
+        load_w1(0, 1, 0, K_PASS, "table1")
+        cast_w1(1, 0, 0, 256, False)
+        cast_w1(1, 0, 256, K_PASS, True, base=256)
         quant_w1(1, 0, 2)
-        load_w1(0, 1, 0, "w_bf00")
-        load_w1(0, 1, 1, "w_raw01")
-        load_w1(1, 1, 0, "w_raw10")
-        load_w1(1, 1, 1, "w_raw11")
-        w4_sb = keep.tile([P, 2, 2 * N], U8, name="w4_sb", tag="w_bf10", align_bytes=64)
 
         def step(i):
             add_climate(i)
@@ -260,25 +258,26 @@ def tile_list_crossdating_match_strength_kernel(
             count_turns(i)
 
         step(0)
-        load_clim(4, 2, "table_sc")
         step(1)
-        cast_w1(0, 1, 0, False)
-        cast_w1(0, 1, 1, False)
+        load_clim(4, "table_sc", False)
+        cast_w1(1, 1, 0, 256, False)
+        cast_w1(1, 1, 256, K_PASS, False)
         step(2)
-        cast_w1(1, 1, 0, False)
-        cast_w1(1, 1, 1, False)
+        cast_w1(0, 1, 0, 256, False)
+        cast_w1(0, 1, 256, K_PASS, False)
         step(3)
-        load_clim(6, 2, "table1")
-        nc.sync.dma_start(out=w4_sb[:].bitcast(I32), in_=w4_words.rearrange("a p c -> p a c").bitcast(I32))
+        load_clim(6, "w_raw0", False)
         for quad in range(4):
             nc.sync.dma_start(
                 out=w4_sc[32 * quad : 32 * quad + 4, :, :].bitcast(I32),
                 in_=w4_scales[:, 4 * quad : 4 * quad + 4, :].rearrange("a r n -> r a n").bitcast(I32),
             )
         pick(0, 0, PAIRS)
-        quant_w1(0, 1)
-        combine(0, 0, PAIRS)
         quant_w1(1, 1)
+        combine(0, 0, PAIRS)
+        quant_w1(0, 1)
+        w4_sb = keep.tile([P, 2, 2 * N], U8, name="w4_sb", tag="w_bf01", align_bytes=64)
+        nc.sync.dma_start(out=w4_sb[:].bitcast(I32), in_=w4_words.rearrange("a p c -> p a c").bitcast(I32))
         for i in range(4, 7):
             pick(i - 3, 0, PAIRS)
             add_climate(i)

@@ -21,10 +21,18 @@ P = 128
 PACK = 4
 K_PASS = P * PACK
 BANK = 512
-HALF = PAIRS // 2
-QUARTER = 128
+SLICES = H // P
+LAST = SLICES - 1
+PER_COLUMN = 16
+SCORE_WIDTH = 128
+WEAVE_WIDTH = 256
+
 PARTS = [(0, 256), (256, 384), (384, 512)]
+FIRST_BANK = {0: 4, 256: 7, 384: 1}
+COUNTED_ON_SCALAR = range(2, LAST)
+
 TURNS = 1.0 / (2.0 * math.pi)
+ROUNDER = 1.5 * 2.0**23
 
 
 def tile_list_crossdating_match_strength_kernel(
@@ -36,54 +44,45 @@ def tile_list_crossdating_match_strength_kernel(
         ring = ctx.enter_context(tc.tile_pool(name="ring", bufs=2))
         psum = ctx.enter_context(tc.psum_pool(name="psum", bufs=1))
 
-        offs_sb = keep.tile([P, S // 16], U16, name="offs_sb")
-        pos1_sb = keep.tile([P, PAIRS // 16], U16, name="pos1_sb")
-        pos2_sb = keep.tile([P, PAIRS // 16], U16, name="pos2_sb")
+        offs_sb = keep.tile([P, S // PER_COLUMN], U16, name="offs_sb")
+        pos1_sb = keep.tile([P, PAIRS // PER_COLUMN], U16, name="pos1_sb")
+        pos2_sb = keep.tile([P, PAIRS // PER_COLUMN], U16, name="pos2_sb")
         table = [keep.tile([P, T], U16, name=f"table{a}", tag=f"table{a}", align_bytes=64) for a in range(2)]
         table_sc = keep.tile([P, T], U8, name="table_sc", tag="table_sc", align_bytes=64)
         v_codes = [keep.tile([P, S], U16, name=f"v_codes{a}", align_bytes=64) for a in range(2)]
         v_sc = [keep.tile([P, S], U8, name=f"v_sc{a}", align_bytes=64) for a in range(2)]
-        w_raw = {}
-        w_bf = {}
-        w_codes = {}
-        w_sc = {}
+        w_bf, w_codes, w_sc = {}, {}, {}
         for b in range(2):
             for a in range(2):
                 w_bf[a, b] = keep.tile([P, PACK * K_PASS], BF16, name=f"w_bf{a}{b}", tag=f"w_bf{a}{b}", align_bytes=64)
                 w_codes[a, b] = keep.tile([P, K_PASS], U32, name=f"w_codes{a}{b}", align_bytes=64)
                 w_sc[a, b] = keep.tile([P, K_PASS], U8, name=f"w_sc{a}{b}", align_bytes=64)
-        clim = {}
         gain_sb = keep.tile([P, 2, PACK], F32, name="gain_sb")
         w4_sc = keep.tile([P, 2, N], U8, name="w4_sc", align_bytes=64)
         minus_half = keep.tile([P, PAIRS], F32, name="minus_half")
-        warm = keep.tile([P, 8], F32, name="warm")
-        warm_out = keep.tile([P, 8], F32, name="warm_out")
-        cosines = [keep.tile([P, S], F32, name=f"cosines{i}") for i in range(8)]
+        cosines = [keep.tile([P, S], F32, name=f"cosines{i}") for i in range(SLICES)]
         z_f32 = [keep.tile([P, PACK, PAIRS], F32, name=f"z_f32{b}") for b in range(2)]
-        z_codes = {}
-        z_sc = {}
-        z_bf = {}
+        z_codes, z_sc = {}, {}
         for b, lo, hi in [(0, 0, PAIRS)] + [(1, lo, hi) for lo, hi in PARTS]:
             z_codes[b, lo] = keep.tile([P, hi - lo], U32, name=f"z_codes{b}{lo}", align_bytes=64)
             z_sc[b, lo] = keep.tile([P, hi - lo], U8, name=f"z_sc{b}{lo}", align_bytes=64)
+        w_raw, clim, phase, turns, master, z_bf, score = {}, {}, {}, {}, {}, {}, {}
 
         nc.vector.memset(table_sc[:].bitcast(I32), 0)
-        nc.vector.memset(warm[:], 0.0)
-        nc.scalar.activation(warm_out[:], warm[:], ACT.Sin)
         nc.vector.memset(v_sc[1][:].bitcast(I32), 0)
         nc.vector.memset(w4_sc[:].rearrange("p a n -> p (a n)").bitcast(I32), 0)
         nc.vector.memset(minus_half[:], -0.5)
 
-        def load_w1(a, b, lo, hi, tag):
-            w_raw[a, b, lo] = keep.tile([P, PACK, hi - lo], F32, name="w_raw", tag=tag, align_bytes=64)
+        def load_w1(a, b, lo, hi, slot):
+            w_raw[a, b, lo] = keep.tile([P, PACK, hi - lo], F32, name="w_raw", tag=slot, align_bytes=64)
             rows = w1[a * K_PASS : (a + 1) * K_PASS, b * K_PASS + lo : b * K_PASS + hi]
             nc.sync.dma_start(out=w_raw[a, b, lo][:], in_=rows.rearrange("(p j) c -> p j c", j=PACK))
 
-        def load_clim(i, tag, split):
+        def load_climate(i, slot, one_by_one):
             b, t = divmod(i, PACK)
             rows = climate[b * K_PASS : (b + 1) * K_PASS, :].rearrange("(p t) j -> p t j", t=PACK)
-            staged = keep.tile([P, 2, S], F32, name="staged", tag=tag, align_bytes=64)
-            if split:
+            staged = keep.tile([P, 2, S], F32, name="staged", tag=slot, align_bytes=64)
+            if one_by_one:
                 for e in range(2):
                     nc.sync.dma_start(out=staged[:, e, :], in_=rows[:, t + e, :])
             else:
@@ -91,32 +90,16 @@ def tile_list_crossdating_match_strength_kernel(
             for e in range(2):
                 clim[i + e] = staged[:, e, :]
 
-        nc.sync.dma_start(offs_sb[:], offs)
-        nc.sync.dma_start(pos1_sb[:], pos1)
-        nc.sync.dma_start(pos2_sb[:], pos2)
-        nc.sync.dma_start(out=gain_sb[:], in_=gain.rearrange("(b p t) -> p b t", b=2, t=PACK))
-        for q in range(4):
-            words = slice(q * 512, (q + 1) * 512)
-            nc.sync.dma_start(out=table[0][:].bitcast(I32)[:, words], in_=tab_words[0].bitcast(I32)[:, words])
-        for r in range(4):
-            nc.sync.dma_start(
-                out=table_sc[r:P:16, :].bitcast(I32),
-                in_=tab_scales.rearrange("a (q r) t -> r q a t", r=4)[r].bitcast(I32),
-            )
-        load_w1(0, 0, 0, K_PASS, "w_raw0")
-        nc.sync.dma_start(out=table[1][:].bitcast(I32), in_=tab_words[1].bitcast(I32))
-        load_w1(1, 0, 0, 256, "w_raw10")
-        load_w1(1, 0, 256, K_PASS, "w_raw11")
-
-        def cast_w1(a, b, lo, hi, on_vector, base=0):
+        def cast_w1(a, b, lo, hi, on_vector, loaded_from=0):
             dst = w_bf[a, b][:].rearrange("p (t m j) -> p m t j", t=PACK, j=PACK)[:, lo // PACK : hi // PACK, :, :]
-            src = w_raw[a, b, base][:, :, lo - base : hi - base].rearrange("p j (m t) -> p m t j", t=PACK)
+            src = w_raw[a, b, loaded_from][:, :, lo - loaded_from : hi - loaded_from]
+            src = src.rearrange("p j (m t) -> p m t j", t=PACK)
             if on_vector:
                 nc.vector.tensor_copy(out=dst, in_=src)
             else:
                 nc.scalar.copy(out=dst, in_=src)
 
-        def quant_w1(a, b, pieces=1):
+        def quantise_w1(a, b, pieces=1):
             width = K_PASS // pieces
             for lo in range(0, K_PASS, width):
                 nc.vector.quantize_mx(
@@ -125,13 +108,15 @@ def tile_list_crossdating_match_strength_kernel(
                     in_=w_bf[a, b][:, PACK * lo : PACK * (lo + width)],
                 )
 
-        phase = {}
-        turns = {}
-
         def add_climate(i):
             b, t = divmod(i, PACK)
             phase[i] = ring.tile([P, S], F32, name="phase", tag="phase", bufs=3)
-            for h in range(2):
+            if i in COUNTED_ON_SCALAR:
+                nc.scalar.activation(clim[i], clim[i], ACT.Copy, scale=TURNS, bias=0.25)
+                scalar, op0 = TURNS, ALU.mult
+            else:
+                scalar, op0 = math.pi / 2, ALU.add
+            for h in range(S // BANK):
                 acc = psum.tile([P, BANK], F32, name="acc", tag=f"bank{(2 * i + h) % 4}")
                 cols = slice(h * BANK, (h + 1) * BANK)
                 for a in range(2):
@@ -145,38 +130,52 @@ def tile_list_crossdating_match_strength_kernel(
                         stop=(a == 1),
                     )
                 nc.vector.scalar_tensor_tensor(
-                    out=phase[i][:, cols], in0=acc[:], scalar=math.pi / 2, in1=clim[i][:, cols], op0=ALU.add, op1=ALU.add
+                    out=phase[i][:, cols], in0=acc[:], scalar=scalar, in1=clim[i][:, cols], op0=op0, op1=ALU.add
                 )
 
         def count_turns(i):
             turns[i] = ring.tile([P, S], I32, name="turns", tag="turns", bufs=2)
-            nc.vector.tensor_scalar(
-                out=turns[i][:], in0=phase[i][:], scalar1=TURNS, scalar2=0.0, op0=ALU.mult, op1=ALU.add
-            )
+            if i in COUNTED_ON_SCALAR:
+                nc.scalar.activation(turns[i][:].bitcast(U32), phase[i][:], ACT.Copy, bias=ROUNDER)
+            else:
+                nc.vector.tensor_scalar(
+                    out=turns[i][:], in0=phase[i][:], scalar1=TURNS, scalar2=0.0, op0=ALU.mult, op1=ALU.add
+                )
 
         def cosine(i):
             b, t = divmod(i, PACK)
             frac = ring.tile([P, S], F32, name="frac", tag="frac", bufs=3)
-            nc.vector.scalar_tensor_tensor(
-                out=frac[:], in0=phase[i][:], scalar=TURNS, in1=turns[i][:], op0=ALU.mult, op1=ALU.subtract
-            )
-            if i == 7:
+            if i in COUNTED_ON_SCALAR:
+                nc.vector.scalar_tensor_tensor(
+                    out=frac[:], in0=turns[i][:], scalar=ROUNDER, in1=phase[i][:], op0=ALU.subtract, op1=ALU.subtract
+                )
+                angle = -2.0 * math.pi
+            else:
+                nc.vector.scalar_tensor_tensor(
+                    out=frac[:], in0=phase[i][:], scalar=TURNS, in1=turns[i][:], op0=ALU.mult, op1=ALU.subtract
+                )
+                angle = 2.0 * math.pi
+            if i == LAST:
                 plain = ring.tile([P, S], F32, name="plain", tag="frac", bufs=3)
-                nc.scalar.activation(plain[:], frac[:], ACT.Sin, scale=2.0 * math.pi)
+                nc.scalar.activation(plain[:], frac[:], ACT.Sin, scale=angle)
                 nc.scalar.activation(cosines[i][:], plain[:], ACT.Copy, scale=gain_sb[:, b, t : t + 1])
             else:
-                nc.scalar.activation(cosines[i][:], frac[:], ACT.Sin, scale=2.0 * math.pi)
+                nc.scalar.activation(cosines[i][:], frac[:], ACT.Sin, scale=angle)
 
-        master = {}
+        def step(i):
+            add_climate(i)
+            if i > 0:
+                cosine(i - 1)
+            count_turns(i)
 
-        def pick(i, lo, hi, after=None):
-            if after is None:
+        def pick(i, lo, hi, slot=None):
+            if slot is None:
                 master[i, lo] = ring.tile([P, PAIRS], F32, name="master", tag="master", bufs=3)
             else:
-                master[i, lo] = keep.tile([P, hi - lo], F32, name="master_late", tag=after, align_bytes=64)
+                master[i, lo] = keep.tile([P, hi - lo], F32, name="master_late", tag=slot, align_bytes=64)
             nc.vector.tensor_tensor(
                 master[i, lo][:, : hi - lo],
-                cosines[i][:].indirect(pos2_sb[:, lo // 16 : hi // 16]),
+                cosines[i][:].indirect(pos2_sb[:, lo // PER_COLUMN : hi // PER_COLUMN]),
                 minus_half[:, : hi - lo],
                 ALU.mult,
             )
@@ -185,51 +184,51 @@ def tile_list_crossdating_match_strength_kernel(
             b, t = divmod(i, PACK)
             dst = z_f32[b][:, t, lo:hi]
             nc.vector.tensor_tensor(
-                dst, cosines[i][:].indirect(pos1_sb[:, lo // 16 : hi // 16]), master[i, lo][:, : hi - lo], ALU.add
+                dst,
+                cosines[i][:].indirect(pos1_sb[:, lo // PER_COLUMN : hi // PER_COLUMN]),
+                master[i, lo][:, : hi - lo],
+                ALU.add,
             )
-            if i != 7:
+            if i != LAST:
                 nc.scalar.activation(dst, dst, ACT.Copy, scale=gain_sb[:, b, t : t + 1])
 
         def weave(b, lo, hi, on_vector):
             z_bf[b, lo] = keep.tile([P, hi - lo, PACK], BF16, name="z_bf", tag=f"z_bf{b}{lo}", align_bytes=64)
-            for m0 in range(lo, hi, HALF):
-                m1 = min(hi, m0 + HALF)
+            for m0 in range(lo, hi, WEAVE_WIDTH):
+                m1 = min(hi, m0 + WEAVE_WIDTH)
                 src = z_f32[b][:, :, m0:m1].rearrange("p t m -> p m t")
                 if on_vector:
                     nc.vector.tensor_copy(out=z_bf[b, lo][:, m0 - lo : m1 - lo, :], in_=src)
                 else:
                     nc.scalar.copy(out=z_bf[b, lo][:, m0 - lo : m1 - lo, :], in_=src)
 
-        def quant_z(b, lo):
+        def quantise_z(b, lo):
             nc.vector.quantize_mx(
                 out=z_codes[b, lo][:].bitcast(FP8X4),
                 scales=z_sc[b, lo][:],
                 in_=z_bf[b, lo][:].rearrange("p m t -> p (m t)"),
             )
 
-        score = {}
-        first_bank = {0: 4, 256: 7, 384: 1}
-
         def score_pass(b, lo, hi):
-            per_bank = 2 if hi - lo == 256 else 3
-            base = 0 if b == 0 else lo
+            per_bank = min(BANK // (hi - lo), N // P // 2)
+            codes_from = 0 if b == 0 else lo
             for g in range(N // P // per_bank):
                 if b == 0:
                     score[lo, g] = psum.tile(
-                        [P, per_bank, hi - lo], F32, name="score", tag=f"bank{(first_bank[lo] + g) % 8}"
+                        [P, per_bank, hi - lo], F32, name="score", tag=f"bank{(FIRST_BANK[lo] + g) % 8}"
                     )
                 for e in range(per_bank):
                     n0 = (per_bank * g + e) * P
-                    for m0 in range(lo, hi, QUARTER):
-                        cols = slice(m0 - base, m0 - base + QUARTER)
+                    for m0 in range(lo, hi, SCORE_WIDTH):
+                        cols = slice(m0 - codes_from, m0 - codes_from + SCORE_WIDTH)
                         nc.tensor.matmul_mx(
-                            out=score[lo, g][:, e, m0 - lo : m0 - lo + QUARTER],
+                            out=score[lo, g][:, e, m0 - lo : m0 - lo + SCORE_WIDTH],
                             lhsT=w4_sb[:, b, 2 * n0 : 2 * (n0 + P)].bitcast(FP4X4),
                             lhsT_scale=w4_sc[:, b, n0 : n0 + P],
-                            rhs=z_codes[b, base][:, cols].bitcast(FP8X4),
-                            rhs_scale=z_sc[b, base][:, cols],
+                            rhs=z_codes[b, codes_from][:, cols].bitcast(FP8X4),
+                            rhs_scale=z_sc[b, codes_from][:, cols],
                             start=(b == 0 and e == 0 and m0 == lo),
-                            stop=(b == 1 and e == per_bank - 1 and m0 + QUARTER == hi),
+                            stop=(b == 1 and e == per_bank - 1 and m0 + SCORE_WIDTH == hi),
                         )
                 if b == 1:
                     strength = ring.tile([P, per_bank, hi - lo], F32, name="strength", tag="strength", bufs=4)
@@ -237,80 +236,109 @@ def tile_list_crossdating_match_strength_kernel(
                     rows = out[per_bank * g * P : per_bank * (g + 1) * P, lo:hi]
                     nc.sync.dma_start(out=rows.rearrange("(e p) m -> p e m", e=per_bank), in_=strength[:])
 
+        nc.sync.dma_start(offs_sb[:], offs)
+        nc.sync.dma_start(pos1_sb[:], pos1)
+        nc.sync.dma_start(pos2_sb[:], pos2)
+        nc.sync.dma_start(out=gain_sb[:], in_=gain.rearrange("(b p t) -> p b t", b=2, t=PACK))
+        piece = T // 2 // 4
+        for q in range(4):
+            words = slice(q * piece, (q + 1) * piece)
+            nc.sync.dma_start(out=table[0][:].bitcast(I32)[:, words], in_=tab_words[0].bitcast(I32)[:, words])
+        for r in range(4):
+            nc.sync.dma_start(
+                out=table_sc[r:P:16, :].bitcast(I32),
+                in_=tab_scales.rearrange("a (q r) t -> r q a t", r=4)[r].bitcast(I32),
+            )
+        half = K_PASS // 2
+        load_w1(0, 0, 0, K_PASS, "w_raw0")
+        nc.sync.dma_start(out=table[1][:].bitcast(I32), in_=tab_words[1].bitcast(I32))
+        load_w1(1, 0, 0, half, "w_raw10")
+        load_w1(1, 0, half, K_PASS, "w_raw11")
+
         nc.vector.tensor_copy(v_codes[0][:], table[0][:].indirect(offs_sb[:]))
         nc.vector.tensor_copy(v_sc[0][:], table_sc[:].indirect(offs_sb[:]))
-        nc.sync.dma_start(out=v_sc[1][0:112, :].bitcast(I32), in_=v_sc[0][16:128, :].bitcast(I32))
-        load_clim(0, "table_sc", True)
+        nc.sync.dma_start(out=v_sc[1][0 : P - 16, :].bitcast(I32), in_=v_sc[0][16:P, :].bitcast(I32))
+        load_climate(0, "table_sc", True)
         cast_w1(0, 0, 0, K_PASS, False)
-        load_clim(2, "w_raw0", True)
-        quant_w1(0, 0)
+        load_climate(2, "w_raw0", True)
+        quantise_w1(0, 0)
         load_w1(1, 1, 0, K_PASS, "w_bf00")
         nc.vector.tensor_copy(v_codes[1][:], table[1][:].indirect(offs_sb[:]))
         load_w1(0, 1, 0, K_PASS, "table1")
-        cast_w1(1, 0, 0, 256, False)
-        cast_w1(1, 0, 256, K_PASS, True, base=256)
-        quant_w1(1, 0, 2)
-
-        def step(i):
-            add_climate(i)
-            if i > 0:
-                cosine(i - 1)
-            count_turns(i)
+        cast_w1(1, 0, 0, half, False)
+        cast_w1(1, 0, half, K_PASS, True, loaded_from=half)
+        quantise_w1(1, 0, pieces=2)
 
         step(0)
         step(1)
-        load_clim(4, "table_sc", False)
-        cast_w1(1, 1, 0, 256, False)
-        cast_w1(1, 1, 256, K_PASS, False)
+        load_climate(4, "table_sc", False)
+        cast_w1(1, 1, 0, half, False)
+        cast_w1(1, 1, half, K_PASS, False)
         step(2)
-        cast_w1(0, 1, 0, 256, False)
-        cast_w1(0, 1, 256, K_PASS, False)
-        step(3)
-        load_clim(6, "w_raw0", False)
-        for quad in range(4):
-            nc.sync.dma_start(
-                out=w4_sc[32 * quad : 32 * quad + 4, :, :].bitcast(I32),
-                in_=w4_scales[:, 4 * quad : 4 * quad + 4, :].rearrange("a r n -> r a n").bitcast(I32),
-            )
+        cast_w1(0, 1, 0, half, False)
+        cast_w1(0, 1, half, K_PASS, False)
         pick(0, 0, PAIRS)
-        quant_w1(1, 1)
+        add_climate(3)
         combine(0, 0, PAIRS)
-        quant_w1(0, 1)
-        w4_sb = keep.tile([P, 2, 2 * N], U8, name="w4_sb", tag="w_bf01", align_bytes=64)
+        cosine(2)
+        count_turns(3)
+        load_climate(6, "w_raw0", False)
+        for q in range(4):
+            nc.sync.dma_start(
+                out=w4_sc[32 * q : 32 * q + 4, :, :].bitcast(I32),
+                in_=w4_scales[:, 4 * q : 4 * q + 4, :].rearrange("a r n -> r a n").bitcast(I32),
+            )
+        pick(1, 0, PAIRS)
+        quantise_w1(1, 1)
+        combine(1, 0, PAIRS)
+        cosine(3)
+        quantise_w1(0, 1)
+        w4_sb = keep.tile([P, 2, 2 * N], U8, name="w4_sb", tag="w_bf11", align_bytes=64)
         nc.sync.dma_start(out=w4_sb[:].bitcast(I32), in_=w4_words.rearrange("a p c -> p a c").bitcast(I32))
-        for i in range(4, 7):
-            pick(i - 3, 0, PAIRS)
-            add_climate(i)
-            combine(i - 3, 0, PAIRS)
-            cosine(i - 1)
-            count_turns(i)
+
+        pick(2, 0, PAIRS, slot="w_bf01")
+        add_climate(4)
+        combine(2, 0, PAIRS)
+        count_turns(4)
+        step(5)
+        pick(3, 0, PAIRS, slot="table_sc")
+        add_climate(6)
+        combine(3, 0, PAIRS)
+        cosine(5)
+        count_turns(6)
         weave(0, 0, PAIRS, False)
-        step(7)
-        work = [(i, lo, hi) for lo, hi in PARTS for i in range(4, 8)]
-        waits = {3: "z_bf00", 8: "z_bf10", 11: "z_bf1256"}
-        last = None
-        for n, item in enumerate(work):
-            if n == 3:
-                quant_z(0, 0)
-                for lo, hi in PARTS:
-                    score_pass(0, lo, hi)
-            if n == 8:
-                quant_z(1, 0)
-                score_pass(1, *PARTS[0])
-            if n == 11:
-                quant_z(1, 256)
-                score_pass(1, *PARTS[1])
-            pick(*item, after=waits.get(n))
-            if n == 0:
-                cosine(7)
-            else:
-                combine(*last)
-            last = item
-            if n == 4:
-                weave(1, *PARTS[0], False)
-            if n == 8:
-                weave(1, *PARTS[1], False)
-        combine(*last)
-        weave(1, *PARTS[2], True)
-        quant_z(1, 384)
-        score_pass(1, *PARTS[2])
+        step(LAST)
+
+        first, second, third = PARTS
+        pick(4, *first)
+        cosine(LAST)
+        for i in (5, 6):
+            pick(i, *first)
+            combine(i - 1, *first)
+        quantise_z(0, 0)
+        for part in PARTS:
+            score_pass(0, *part)
+        pick(LAST, *first, slot="z_bf00")
+        combine(6, *first)
+        pick(4, *second)
+        combine(LAST, *first)
+        weave(1, *first, False)
+        for i in (5, 6, LAST):
+            pick(i, *second)
+            combine(i - 1, *second)
+        quantise_z(1, first[0])
+        score_pass(1, *first)
+        pick(4, *third, slot=f"z_bf1{first[0]}")
+        combine(LAST, *second)
+        weave(1, *second, False)
+        for i in (5, 6):
+            pick(i, *third)
+            combine(i - 1, *third)
+        quantise_z(1, second[0])
+        score_pass(1, *second)
+        pick(LAST, *third, slot=f"z_bf1{second[0]}")
+        combine(6, *third)
+        combine(LAST, *third)
+        weave(1, *third, True)
+        quantise_z(1, third[0])
+        score_pass(1, *third)

import math
from contextlib import ExitStack

import concourse.mybir as mybir

T, S, PAIRS, K, H, N = 4096, 1024, 512, 1024, 1024, 768
FLOPS = 2 * K * H * S + 2 * H * N * PAIRS

F32 = mybir.dt.float32
BF16 = mybir.dt.bfloat16
I32 = mybir.dt.int32
U32 = mybir.dt.uint32
U16 = mybir.dt.uint16
U8 = mybir.dt.uint8
FP8X4 = mybir.dt.float8_e4m3fn_x4
FP4X4 = mybir.dt.float4_e2m1fn_x4
ALU = mybir.AluOpType
ACT = mybir.ActivationFunctionType

P = 128
PACK = 4
K_PASS = P * PACK
BANK = 512
SLICES = H // P
LAST = SLICES - 1
PER_COLUMN = 16
SCORE_WIDTH = 128
WEAVE_WIDTH = 256

PARTS = [(0, 256), (256, 384), (384, 512)]
FIRST_BANK = {0: 4, 256: 7, 384: 1}
COUNTED_ON_SCALAR = range(2, LAST)

TURNS = 1.0 / (2.0 * math.pi)
ROUNDER = 1.5 * 2.0**23


def tile_list_crossdating_match_strength_kernel(
    tc, tab_words, tab_scales, offs, pos1, pos2, w1, climate, gain, w4_words, w4_scales, out
):
    nc = tc.nc
    with ExitStack() as ctx:
        keep = ctx.enter_context(tc.tile_pool(name="keep", bufs=1))
        ring = ctx.enter_context(tc.tile_pool(name="ring", bufs=2))
        psum = ctx.enter_context(tc.psum_pool(name="psum", bufs=1))

        offs_sb = keep.tile([P, S // PER_COLUMN], U16, name="offs_sb")
        pos1_sb = keep.tile([P, PAIRS // PER_COLUMN], U16, name="pos1_sb")
        pos2_sb = keep.tile([P, PAIRS // PER_COLUMN], U16, name="pos2_sb")
        table = [keep.tile([P, T], U16, name=f"table{a}", tag=f"table{a}", align_bytes=64) for a in range(2)]
        table_sc = keep.tile([P, T], U8, name="table_sc", tag="table_sc", align_bytes=64)
        v_codes = [keep.tile([P, S], U16, name=f"v_codes{a}", align_bytes=64) for a in range(2)]
        v_sc = [keep.tile([P, S], U8, name=f"v_sc{a}", align_bytes=64) for a in range(2)]
        w_bf, w_codes, w_sc = {}, {}, {}
        for b in range(2):
            for a in range(2):
                w_bf[a, b] = keep.tile([P, PACK * K_PASS], BF16, name=f"w_bf{a}{b}", tag=f"w_bf{a}{b}", align_bytes=64)
                w_codes[a, b] = keep.tile([P, K_PASS], U32, name=f"w_codes{a}{b}", align_bytes=64)
                w_sc[a, b] = keep.tile([P, K_PASS], U8, name=f"w_sc{a}{b}", align_bytes=64)
        gain_sb = keep.tile([P, 2, PACK], F32, name="gain_sb")
        w4_sc = keep.tile([P, 2, N], U8, name="w4_sc", align_bytes=64)
        minus_half = keep.tile([P, PAIRS], F32, name="minus_half")
        cosines = [keep.tile([P, S], F32, name=f"cosines{i}") for i in range(SLICES)]
        z_f32 = [keep.tile([P, PACK, PAIRS], F32, name=f"z_f32{b}") for b in range(2)]
        z_codes, z_sc = {}, {}
        for b, lo, hi in [(0, 0, PAIRS)] + [(1, lo, hi) for lo, hi in PARTS]:
            z_codes[b, lo] = keep.tile([P, hi - lo], U32, name=f"z_codes{b}{lo}", align_bytes=64)
            z_sc[b, lo] = keep.tile([P, hi - lo], U8, name=f"z_sc{b}{lo}", align_bytes=64)
        w_raw, clim, phase, turns, master, z_bf, score = {}, {}, {}, {}, {}, {}, {}

        nc.vector.memset(table_sc[:].bitcast(I32), 0)
        nc.vector.memset(v_sc[1][:].bitcast(I32), 0)
        nc.vector.memset(w4_sc[:].rearrange("p a n -> p (a n)").bitcast(I32), 0)
        nc.vector.memset(minus_half[:], -0.5)

        def load_w1(a, b, lo, hi, slot):
            w_raw[a, b, lo] = keep.tile([P, PACK, hi - lo], F32, name="w_raw", tag=slot, align_bytes=64)
            rows = w1[a * K_PASS : (a + 1) * K_PASS, b * K_PASS + lo : b * K_PASS + hi]
            nc.sync.dma_start(out=w_raw[a, b, lo][:], in_=rows.rearrange("(p j) c -> p j c", j=PACK))

        def load_climate(i, slot, one_by_one):
            b, t = divmod(i, PACK)
            rows = climate[b * K_PASS : (b + 1) * K_PASS, :].rearrange("(p t) j -> p t j", t=PACK)
            staged = keep.tile([P, 2, S], F32, name="staged", tag=slot, align_bytes=64)
            if one_by_one:
                for e in range(2):
                    nc.sync.dma_start(out=staged[:, e, :], in_=rows[:, t + e, :])
            else:
                nc.sync.dma_start(out=staged[:], in_=rows[:, t : t + 2, :])
            for e in range(2):
                clim[i + e] = staged[:, e, :]

        def cast_w1(a, b, lo, hi, on_vector, loaded_from=0):
            dst = w_bf[a, b][:].rearrange("p (t m j) -> p m t j", t=PACK, j=PACK)[:, lo // PACK : hi // PACK, :, :]
            src = w_raw[a, b, loaded_from][:, :, lo - loaded_from : hi - loaded_from]
            src = src.rearrange("p j (m t) -> p m t j", t=PACK)
            if on_vector:
                nc.vector.tensor_copy(out=dst, in_=src)
            else:
                nc.scalar.copy(out=dst, in_=src)

        def quantise_w1(a, b, pieces=1):
            width = K_PASS // pieces
            for lo in range(0, K_PASS, width):
                nc.vector.quantize_mx(
                    out=w_codes[a, b][:, lo : lo + width].bitcast(FP8X4),
                    scales=w_sc[a, b][:, lo : lo + width],
                    in_=w_bf[a, b][:, PACK * lo : PACK * (lo + width)],
                )

        def add_climate(i):
            b, t = divmod(i, PACK)
            phase[i] = ring.tile([P, S], F32, name="phase", tag="phase", bufs=3)
            if i in COUNTED_ON_SCALAR:
                nc.scalar.activation(clim[i], clim[i], ACT.Copy, scale=TURNS, bias=0.25)
                scalar, op0 = TURNS, ALU.mult
            else:
                scalar, op0 = math.pi / 2, ALU.add
            for h in range(S // BANK):
                acc = psum.tile([P, BANK], F32, name="acc", tag=f"bank{(2 * i + h) % 4}")
                cols = slice(h * BANK, (h + 1) * BANK)
                for a in range(2):
                    nc.tensor.matmul_mx(
                        out=acc[:],
                        lhsT=w_codes[a, b][:, t * P : (t + 1) * P].bitcast(FP8X4),
                        lhsT_scale=w_sc[a, b][:, t * P : (t + 1) * P],
                        rhs=v_codes[a][:, cols].bitcast(FP4X4),
                        rhs_scale=v_sc[a][:, cols],
                        start=(a == 0),
                        stop=(a == 1),
                    )
                nc.vector.scalar_tensor_tensor(
                    out=phase[i][:, cols], in0=acc[:], scalar=scalar, in1=clim[i][:, cols], op0=op0, op1=ALU.add
                )

        def count_turns(i):
            turns[i] = ring.tile([P, S], I32, name="turns", tag="turns", bufs=2)
            if i in COUNTED_ON_SCALAR:
                nc.scalar.activation(turns[i][:].bitcast(U32), phase[i][:], ACT.Copy, bias=ROUNDER)
            else:
                nc.vector.tensor_scalar(
                    out=turns[i][:], in0=phase[i][:], scalar1=TURNS, scalar2=0.0, op0=ALU.mult, op1=ALU.add
                )

        def cosine(i):
            b, t = divmod(i, PACK)
            frac = ring.tile([P, S], F32, name="frac", tag="frac", bufs=3)
            if i in COUNTED_ON_SCALAR:
                nc.vector.scalar_tensor_tensor(
                    out=frac[:], in0=turns[i][:], scalar=ROUNDER, in1=phase[i][:], op0=ALU.subtract, op1=ALU.subtract
                )
                angle = -2.0 * math.pi
            else:
                nc.vector.scalar_tensor_tensor(
                    out=frac[:], in0=phase[i][:], scalar=TURNS, in1=turns[i][:], op0=ALU.mult, op1=ALU.subtract
                )
                angle = 2.0 * math.pi
            if i == LAST:
                plain = ring.tile([P, S], F32, name="plain", tag="frac", bufs=3)
                nc.scalar.activation(plain[:], frac[:], ACT.Sin, scale=angle)
                nc.scalar.activation(cosines[i][:], plain[:], ACT.Copy, scale=gain_sb[:, b, t : t + 1])
            else:
                nc.scalar.activation(cosines[i][:], frac[:], ACT.Sin, scale=angle)

        def step(i):
            add_climate(i)
            if i > 0:
                cosine(i - 1)
            count_turns(i)

        def pick(i, lo, hi, slot=None):
            if slot is None:
                master[i, lo] = ring.tile([P, PAIRS], F32, name="master", tag="master", bufs=3)
            else:
                master[i, lo] = keep.tile([P, hi - lo], F32, name="master_late", tag=slot, align_bytes=64)
            nc.vector.tensor_tensor(
                master[i, lo][:, : hi - lo],
                cosines[i][:].indirect(pos2_sb[:, lo // PER_COLUMN : hi // PER_COLUMN]),
                minus_half[:, : hi - lo],
                ALU.mult,
            )

        def combine(i, lo, hi):
            b, t = divmod(i, PACK)
            dst = z_f32[b][:, t, lo:hi]
            nc.vector.tensor_tensor(
                dst,
                cosines[i][:].indirect(pos1_sb[:, lo // PER_COLUMN : hi // PER_COLUMN]),
                master[i, lo][:, : hi - lo],
                ALU.add,
            )
            if i != LAST:
                nc.scalar.activation(dst, dst, ACT.Copy, scale=gain_sb[:, b, t : t + 1])

        def weave(b, lo, hi, on_vector):
            z_bf[b, lo] = keep.tile([P, hi - lo, PACK], BF16, name="z_bf", tag=f"z_bf{b}{lo}", align_bytes=64)
            for m0 in range(lo, hi, WEAVE_WIDTH):
                m1 = min(hi, m0 + WEAVE_WIDTH)
                src = z_f32[b][:, :, m0:m1].rearrange("p t m -> p m t")
                if on_vector:
                    nc.vector.tensor_copy(out=z_bf[b, lo][:, m0 - lo : m1 - lo, :], in_=src)
                else:
                    nc.scalar.copy(out=z_bf[b, lo][:, m0 - lo : m1 - lo, :], in_=src)

        def quantise_z(b, lo):
            nc.vector.quantize_mx(
                out=z_codes[b, lo][:].bitcast(FP8X4),
                scales=z_sc[b, lo][:],
                in_=z_bf[b, lo][:].rearrange("p m t -> p (m t)"),
            )

        def score_pass(b, lo, hi):
            per_bank = min(BANK // (hi - lo), N // P // 2)
            codes_from = 0 if b == 0 else lo
            for g in range(N // P // per_bank):
                if b == 0:
                    score[lo, g] = psum.tile(
                        [P, per_bank, hi - lo], F32, name="score", tag=f"bank{(FIRST_BANK[lo] + g) % 8}"
                    )
                for e in range(per_bank):
                    n0 = (per_bank * g + e) * P
                    for m0 in range(lo, hi, SCORE_WIDTH):
                        cols = slice(m0 - codes_from, m0 - codes_from + SCORE_WIDTH)
                        nc.tensor.matmul_mx(
                            out=score[lo, g][:, e, m0 - lo : m0 - lo + SCORE_WIDTH],
                            lhsT=w4_sb[:, b, 2 * n0 : 2 * (n0 + P)].bitcast(FP4X4),
                            lhsT_scale=w4_sc[:, b, n0 : n0 + P],
                            rhs=z_codes[b, codes_from][:, cols].bitcast(FP8X4),
                            rhs_scale=z_sc[b, codes_from][:, cols],
                            start=(b == 0 and e == 0 and m0 == lo),
                            stop=(b == 1 and e == per_bank - 1 and m0 + SCORE_WIDTH == hi),
                        )
                if b == 1:
                    strength = ring.tile([P, per_bank, hi - lo], F32, name="strength", tag="strength", bufs=4)
                    nc.scalar.activation(strength[:], score[lo, g][:], ACT.Abs)
                    rows = out[per_bank * g * P : per_bank * (g + 1) * P, lo:hi]
                    nc.sync.dma_start(out=rows.rearrange("(e p) m -> p e m", e=per_bank), in_=strength[:])

        nc.sync.dma_start(offs_sb[:], offs)
        nc.sync.dma_start(pos1_sb[:], pos1)
        nc.sync.dma_start(pos2_sb[:], pos2)
        nc.sync.dma_start(out=gain_sb[:], in_=gain.rearrange("(b p t) -> p b t", b=2, t=PACK))
        piece = T // 2 // 4
        for q in range(4):
            words = slice(q * piece, (q + 1) * piece)
            nc.sync.dma_start(out=table[0][:].bitcast(I32)[:, words], in_=tab_words[0].bitcast(I32)[:, words])
        for r in range(4):
            nc.sync.dma_start(
                out=table_sc[r:P:16, :].bitcast(I32),
                in_=tab_scales.rearrange("a (q r) t -> r q a t", r=4)[r].bitcast(I32),
            )
        half = K_PASS // 2
        load_w1(0, 0, 0, K_PASS, "w_raw0")
        nc.sync.dma_start(out=table[1][:].bitcast(I32), in_=tab_words[1].bitcast(I32))
        load_w1(1, 0, 0, half, "w_raw10")
        load_w1(1, 0, half, K_PASS, "w_raw11")

        nc.vector.tensor_copy(v_codes[0][:], table[0][:].indirect(offs_sb[:]))
        nc.vector.tensor_copy(v_sc[0][:], table_sc[:].indirect(offs_sb[:]))
        nc.sync.dma_start(out=v_sc[1][0 : P - 16, :].bitcast(I32), in_=v_sc[0][16:P, :].bitcast(I32))
        load_climate(0, "table_sc", True)
        cast_w1(0, 0, 0, K_PASS, False)
        load_climate(2, "w_raw0", True)
        quantise_w1(0, 0)
        load_w1(1, 1, 0, K_PASS, "w_bf00")
        nc.vector.tensor_copy(v_codes[1][:], table[1][:].indirect(offs_sb[:]))
        load_w1(0, 1, 0, K_PASS, "table1")
        cast_w1(1, 0, 0, half, False)
        cast_w1(1, 0, half, K_PASS, True, loaded_from=half)
        quantise_w1(1, 0, pieces=2)

        step(0)
        step(1)
        load_climate(4, "table_sc", False)
        cast_w1(1, 1, 0, half, False)
        cast_w1(1, 1, half, K_PASS, False)
        step(2)
        cast_w1(0, 1, 0, half, False)
        cast_w1(0, 1, half, K_PASS, False)
        pick(0, 0, PAIRS)
        add_climate(3)
        combine(0, 0, PAIRS)
        cosine(2)
        count_turns(3)
        load_climate(6, "w_raw0", False)
        for q in range(4):
            nc.sync.dma_start(
                out=w4_sc[32 * q : 32 * q + 4, :, :].bitcast(I32),
                in_=w4_scales[:, 4 * q : 4 * q + 4, :].rearrange("a r n -> r a n").bitcast(I32),
            )
        pick(1, 0, PAIRS)
        quantise_w1(1, 1)
        combine(1, 0, PAIRS)
        cosine(3)
        quantise_w1(0, 1)
        w4_sb = keep.tile([P, 2, 2 * N], U8, name="w4_sb", tag="w_bf11", align_bytes=64)
        nc.sync.dma_start(out=w4_sb[:].bitcast(I32), in_=w4_words.rearrange("a p c -> p a c").bitcast(I32))

        pick(2, 0, PAIRS, slot="w_bf01")
        add_climate(4)
        combine(2, 0, PAIRS)
        count_turns(4)
        step(5)
        pick(3, 0, PAIRS, slot="table_sc")
        add_climate(6)
        combine(3, 0, PAIRS)
        cosine(5)
        count_turns(6)
        weave(0, 0, PAIRS, False)
        step(LAST)

        first, second, third = PARTS
        pick(4, *first)
        cosine(LAST)
        for i in (5, 6):
            pick(i, *first)
            combine(i - 1, *first)
        quantise_z(0, 0)
        for part in PARTS:
            score_pass(0, *part)
        pick(LAST, *first, slot="z_bf00")
        combine(6, *first)
        pick(4, *second)
        combine(LAST, *first)
        weave(1, *first, False)
        for i in (5, 6, LAST):
            pick(i, *second)
            combine(i - 1, *second)
        quantise_z(1, first[0])
        score_pass(1, *first)
        pick(4, *third, slot=f"z_bf1{first[0]}")
        combine(LAST, *second)
        weave(1, *second, False)
        for i in (5, 6):
            pick(i, *third)
            combine(i - 1, *third)
        quantise_z(1, second[0])
        score_pass(1, *second)
        pick(LAST, *third, slot=f"z_bf1{second[0]}")
        combine(6, *third)
        combine(LAST, *third)
        weave(1, *third, True)
        quantise_z(1, third[0])
        score_pass(1, *third)
